import numpy as np
import ml_dtypes


def mxq(x, axis, fmt="e4m3"):
    dtype, down = {"e4m3": (ml_dtypes.float8_e4m3fn, 7), "e5m2": (ml_dtypes.float8_e5m2, 14)}[fmt]
    v = np.moveaxis(np.asarray(x, np.float32).astype(ml_dtypes.bfloat16).astype(np.float64), axis, -1)
    blocks = v.reshape(v.shape[:-1] + (-1, 32))
    amax = np.abs(blocks).max(-1, keepdims=True)
    byte = np.maximum(np.where(amax > 0, np.frexp(amax)[1] - 1 + 127, 0) - down, 1)
    scale = np.exp2(byte - 127.0)
    codes = (blocks / scale).astype(np.float32).astype(dtype).astype(np.float64)
    return np.moveaxis((codes * scale).reshape(v.shape), -1, axis)


WIDE = False


def mx_kscale(k):
    if not WIDE:
        return np.ones(k)
    levels = np.array([10, -10, 5, -5, 0])
    if k % 512:
        return np.exp2(np.random.permutation(np.resize(levels, k // 32))).repeat(32)
    a = np.empty((k // 512, 16))
    for p in range(k // 512):
        a[p, :8] = np.random.permutation(np.resize(levels, 8))
        for g in range(8):
            far = levels[np.abs(levels - a[p, g]) >= 10]
            a[p, g + 8] = far[np.random.randint(len(far))]
    return np.exp2(a.ravel()).repeat(32)


def f64(x):
    return np.asarray(x).astype(np.float64)


def striped(idx):
    return np.tile(idx.reshape(-1, 16).T, (8, 1)).astype(np.uint16)


def unstriped(offs):
    return offs[:16].T.reshape(-1).astype(np.int64)


def striped8(idx):
    return np.concatenate([x.reshape(-1, 16).T for x in idx]).astype(np.uint16)


def runs(offs, k):
    lists = np.stack([offs[16 * r : 16 * r + 16].T.reshape(-1) for r in range(8)]).astype(np.int64)
    return lists[np.arange(k) % 512 // 64]


def pack_weight(w):
    k, n = w.shape
    w = f64(np.asarray(w, np.float32).astype(ml_dtypes.bfloat16)).reshape(k // 32, 32, n)
    amax = np.abs(w).max(1)
    byte = np.clip(np.where(amax > 0, np.frexp(amax)[1] - 1 + 127 - 7, 1), 1, 254)
    scaled = (w * np.exp2(127.0 - byte)[:, None, :]).reshape(k, n).astype(np.float32)
    words = np.ascontiguousarray(scaled.reshape(k // 512, 128, 4, n).transpose(0, 1, 3, 2)).astype(ml_dtypes.float8_e4m3fn).view(np.uint8)
    return words, np.ascontiguousarray(byte.astype(np.uint8).reshape(k // 512, 16, n))


def unpack_weight(words, scales):
    g, p, n, _ = words.shape
    vals = np.ascontiguousarray(words).view(ml_dtypes.float8_e4m3fn).astype(np.float64) * np.repeat(np.exp2(scales.astype(np.float64) - 127.0), 8, axis=1)[..., None]
    return vals.transpose(0, 1, 3, 2).reshape(g * 512, n)


def relu(v):
    return np.maximum(v, 0.0)


K, T, S, V, G, H = 512, 2048, 1024, 512, 2048, 512


def setup_inputs():
    n = np.random.standard_normal
    s = mx_kscale(K)[:, None]
    packed_xT = pack_weight(n((K, T)) * s)
    packed_dT = pack_weight(n((K, G)) / s)
    return {
        "x_words": packed_xT[0],
        "x_scales": packed_xT[1],
        "d_words": packed_dT[0],
        "d_scales": packed_dT[1],
        "gs": (np.random.uniform(0.5, 1.5, (K, 1)) * s).astype(np.float32),
        "offs": striped(np.random.permutation(T)[:S]),
        "k1": striped8(np.random.randint(0, G, (8, H))),
        "l1": striped8(np.stack([np.random.permutation(S)[:V] for _ in range(8)])),
        "r1": striped8(np.stack([np.random.permutation(S)[:V] for _ in range(8)])),
        "k2": striped8(np.random.randint(0, G, (8, H))),
        "k3": striped8(np.random.randint(0, G, (8, H))),
    }


def reference(x_words, x_scales, d_words, d_scales, gs, offs, k1, l1, r1, k2, k3):
    d_k2 = unpack_weight(d_words, d_scales)[np.arange(K)[:, None], runs(k2, K)]
    d_k1 = unpack_weight(d_words, d_scales)[np.arange(K)[:, None], runs(k1, K)]
    xq = unpack_weight(x_words, x_scales)[:, unstriped(offs)]
    h = relu(0.0625 * (d_k1.T @ xq))
    z = f64(gs) * (h[np.arange(H)[:, None], runs(l1, H)])
    d_k3 = unpack_weight(d_words, d_scales)[np.arange(K)[:, None], runs(k3, K)]
    z2 = f64(gs) * (h[np.arange(H)[:, None], runs(r1, H)])
    return 0.0625 * ((d_k2.T @ mxq(z, 0, "e4m3")) + (d_k3.T @ mxq(z2, 0, "e4m3")))

@@ -1,0 +1,205 @@
+from contextlib import ExitStack
+
+import concourse.mybir as mybir
+
+K, T, S, V, G, H = 512, 2048, 1024, 512, 2048, 512
+FLOPS = 2 * K * H * S + 2 * 2 * H * H * V
+
+F32 = mybir.dt.float32
+BF16 = mybir.dt.bfloat16
+I32 = mybir.dt.int32
+U32 = mybir.dt.uint32
+U16 = mybir.dt.uint16
+U8 = mybir.dt.uint8
+FP8X4 = mybir.dt.float8_e4m3fn_x4
+ACT = mybir.ActivationFunctionType
+ALU = mybir.AluOpType
+
+P = 128
+PACK = 4
+LANES = 16
+BANK = 512
+HALF = V // 2
+
+
+def tile_picked_pqtree_relu_p_kernel(
+    tc, x_words, x_scales, d_words, d_scales, gs, offs, k1, l1, r1, k2, k3, out
+):
+    nc = tc.nc
+    with ExitStack() as ctx:
+        lists = ctx.enter_context(tc.tile_pool(name="lists", bufs=1))
+        keep = ctx.enter_context(tc.tile_pool(name="keep", bufs=1))
+        late = ctx.enter_context(tc.tile_pool(name="late", bufs=1))
+        ring = ctx.enter_context(tc.tile_pool(name="ring", bufs=2))
+        psum = ctx.enter_context(tc.psum_pool(name="psum", bufs=8))
+
+        def load_list(name, src):
+            tile = lists.tile(list(src.shape), U16, name=name)
+            nc.sync.dma_start(tile[:], src)
+            return tile
+
+        def load_words(name, src):
+            tile = keep.tile([P, src.shape[2]], U32, name=name, tag=name, align_bytes=64)
+            nc.sync.dma_start(tile[:].bitcast(I32), src[0].rearrange("p n t -> p (n t)").bitcast(I32))
+            return tile
+
+        def zeroed_bytes(name, width):
+            tile = keep.tile([P, width], U8, name=name, tag=name, align_bytes=64)
+            nc.vector.memset(tile[:].bitcast(I32), 0)
+            return tile
+
+        def gather(dst, window, offsets):
+            nc.vector.tensor_copy(dst, window[:].indirect(offsets))
+
+        def place_scale_rows(dst, src):
+            for i in range(4):
+                nc.sync.dma_start(dst[i:P:32, :].bitcast(I32), src[8 * i : P : 32, :].bitcast(I32))
+
+        d_bytes = zeroed_bytes("d_bytes", G)
+        x_bytes = zeroed_bytes("x_bytes", T)
+        k1_list = load_list("k1_list", k1)
+        nc.scalar.dma_start(d_bytes[0:P:8, :].bitcast(I32), d_scales[0].bitcast(I32))
+        offs_list = load_list("offs_list", offs)
+        for q in range(4):
+            nc.scalar.dma_start(
+                x_bytes[32 * q : 32 * q + 4, :].bitcast(I32), x_scales[0, 4 * q : 4 * q + 4, :].bitcast(I32)
+            )
+        k2_list = load_list("k2_list", k2)
+        k3_list = load_list("k3_list", k3)
+        l1_list = load_list("l1_list", l1)
+        r1_list = load_list("r1_list", r1)
+        x_table = load_words("x_table", x_words)
+        d_table = load_words("d_table", d_words)
+        gain = keep.tile([P, PACK], F32, name="gain")
+        nc.gpsimd.dma_start(gain[:], gs.rearrange("(p t) o -> p (t o)", t=PACK))
+        w1_scales = zeroed_bytes("w1_scales", H)
+        w23_scales = zeroed_bytes("w23_scales", 2 * H)
+
+        gain16 = keep.tile([P, PACK], F32, name="gain16")
+        nc.scalar.activation(gain16[:], gain[:], ACT.Copy, scale=0.0625)
+
+        cols = BANK // LANES
+        w1_bytes = keep.tile([P, H], U8, name="w1_bytes", align_bytes=64)
+        gather(w1_bytes[:], d_bytes, k1_list[:])
+        xq_scales0 = keep.tile([P, BANK], U8, name="xq_scales0", align_bytes=64)
+        gather(xq_scales0[:], x_bytes, offs_list[:, 0:cols])
+        w1_bytes_dealt = keep.tile([P, H], U8, name="w1_bytes_dealt", align_bytes=64)
+        nc.vector.tensor_copy(
+            w1_bytes_dealt[:].rearrange("p (t m) -> p t m", t=PACK),
+            w1_bytes[:].rearrange("p (m t) -> p t m", t=PACK),
+        )
+        place_scale_rows(w1_scales, w1_bytes_dealt)
+        xq_words0 = keep.tile([P, BANK], U32, name="xq_words0", align_bytes=64)
+        gather(xq_words0[:], x_table, offs_list[:, 0:cols])
+
+        w1_words = late.tile([P, H], U32, name="w1_words", align_bytes=64, offset=0)
+        gather(w1_words[:], d_table, k1_list[:])
+        w1_dealt = keep.tile([P, H], U32, name="w1_dealt", align_bytes=64)
+        nc.vector.tensor_copy(
+            w1_dealt[:].rearrange("p (t m) -> p t m", t=PACK),
+            w1_words[:].rearrange("p (m t) -> p t m", t=PACK),
+        )
+        xq_scales1 = late.tile([P, BANK], U8, name="xq_scales1", align_bytes=64, offset=0)
+        xq_words1 = late.tile([P, BANK], U32, name="xq_words1", align_bytes=64, offset=BANK)
+        gather(xq_scales1[:], x_bytes, offs_list[:, cols : 2 * cols])
+        gather(xq_words1[:], x_table, offs_list[:, cols : 2 * cols])
+        xq_scales = (xq_scales0, xq_scales1)
+        xq_words = (xq_words0, xq_words1)
+
+        weighted = [keep.tile([P, S], F32, name="weighted%d" % t, align_bytes=64) for t in range(PACK)]
+
+        def first_product(t, j, positive):
+            m = slice(P * t, P * (t + 1))
+            bank = psum.tile([P, BANK], F32, name="h_bank", tag="bank")
+            nc.tensor.matmul_mx(
+                out=bank[:],
+                lhsT=w1_dealt[:, m].bitcast(FP8X4),
+                lhsT_scale=w1_scales[:, m],
+                rhs=xq_words[j][:].bitcast(FP8X4),
+                rhs_scale=xq_scales[j][:],
+                start=True,
+                stop=True,
+            )
+            nc.scalar.activation(positive[:], bank[:], ACT.Relu)
+            nc.scalar.activation(
+                weighted[t][:, BANK * j : BANK * (j + 1)], positive[:], ACT.Copy, scale=gain16[:, t : t + 1]
+            )
+
+        for t, j in ((0, 0), (1, 0), (0, 1), (1, 1), (2, 0), (2, 1), (3, 0)):
+            first_product(t, j, ring.tile([P, BANK], F32, name="positive"))
+        first_product(3, 1, keep.tile([P, BANK], F32, name="last_positive", tag="last_positive", align_bytes=64))
+
+        w23_bytes = keep.tile([P, 2 * H], U8, name="w23_bytes", tag="x_bytes", align_bytes=64)
+        w23_words = keep.tile([P, 2 * H], U32, name="w23_words", tag="x_table", align_bytes=64)
+        for a, lst in enumerate((k2_list, k3_list)):
+            gather(w23_bytes[:, H * a : H * (a + 1)], d_bytes, lst[:])
+        place_scale_rows(w23_scales, w23_bytes)
+        for a, lst in enumerate((k2_list, k3_list)):
+            gather(w23_words[:, H * a : H * (a + 1)], d_table, lst[:])
+
+        hcols = HALF // LANES
+        left_planes = keep.tile([P, PACK, V], BF16, name="left_planes", tag="left_planes", align_bytes=64)
+        right_planes = keep.tile([P, PACK, HALF], BF16, name="right_planes", tag="last_positive", align_bytes=64)
+
+        def weave(name, planes):
+            woven = keep.tile([P, HALF, PACK], BF16, name="woven_" + name, align_bytes=64)
+            nc.scalar.copy(woven[:], planes.rearrange("p t v -> p v t"))
+            return woven
+
+        def quantise(name, woven):
+            words = keep.tile([P, HALF], U32, name="z_words_" + name, align_bytes=64)
+            scales = keep.tile([P, HALF], U8, name="z_scales_" + name, align_bytes=64)
+            nc.vector.quantize_mx(
+                out=words[:].bitcast(FP8X4), scales=scales[:], in_=woven[:].rearrange("p v t -> p (v t)")
+            )
+            return words, scales
+
+        def second_pass(a, banks, z):
+            for m, bank in enumerate(banks):
+                m0 = H * a + P * m
+                nc.tensor.matmul_mx(
+                    out=bank[:],
+                    lhsT=w23_words[:, m0 : m0 + P].bitcast(FP8X4),
+                    lhsT_scale=w23_scales[:, m0 : m0 + P],
+                    rhs=z[0][:].bitcast(FP8X4),
+                    rhs_scale=z[1][:],
+                    start=(a == 0),
+                    stop=(a == 1),
+                )
+
+        def finish(b, banks):
+            for pair in range(2):
+                result = keep.tile([P, 2, HALF], F32, name="result%d%d" % (b, pair))
+                nc.scalar.activation(result[:, 0, :], banks[2 * pair][:], ACT.Copy, scale=0.0625)
+                if b == 0:
+                    nc.scalar.activation(result[:, 1, :], banks[2 * pair + 1][:], ACT.Copy, scale=0.0625)
+                else:
+                    nc.vector.tensor_scalar(result[:, 1, :], banks[2 * pair + 1][:], 0.0625, None, ALU.mult)
+                rows = out[2 * P * pair : 2 * P * (pair + 1), HALF * b : HALF * (b + 1)]
+                nc.sync.dma_start(rows.rearrange("(u p) v -> p u v", p=P), result[:])
+
+        banks = [[psum.tile([P, HALF], F32, name="o_bank", tag="bank") for m in range(4)] for b in range(2)]
+
+        for t in range(PACK):
+            gather(left_planes[:, t, :], weighted[t], l1_list[:])
+        woven_l0 = weave("l0", left_planes[:, :, 0:HALF])
+        woven_l1 = weave("l1", left_planes[:, :, HALF:V])
+        for t in range(PACK):
+            gather(right_planes[:, t, :], weighted[t], r1_list[:, 0:hcols])
+        woven_r0 = weave("r0", right_planes[:])
+        second_pass(0, banks[0], quantise("l0", woven_l0))
+        second_pass(0, banks[1], quantise("l1", woven_l1))
+
+        woven_r1 = keep.tile([P, HALF, PACK], BF16, name="woven_r1", align_bytes=64)
+        low_planes = keep.tile([P, 2, HALF], BF16, name="low_planes", tag="left_planes", align_bytes=64)
+        for t in range(2):
+            gather(low_planes[:, t, :], weighted[t], r1_list[:, hcols : 2 * hcols])
+        nc.scalar.copy(woven_r1[:, :, 0:2], low_planes[:].rearrange("p t v -> p v t"))
+        second_pass(1, banks[0], quantise("r0", woven_r0))
+        high_planes = keep.tile([P, 2, HALF], BF16, name="high_planes", tag="last_positive", align_bytes=64)
+        for t in range(2):
+            gather(high_planes[:, t, :], weighted[2 + t], r1_list[:, hcols : 2 * hcols])
+        finish(0, banks[0])
+        nc.vector.tensor_copy(woven_r1[:, :, 2:4], high_planes[:].rearrange("p t v -> p v t"))
+        second_pass(1, banks[1], quantise("r1", woven_r1))
+        finish(1, banks[1])

@@ -52,26 +52,29 @@ def tile_picked_pqtree_relu_p_kernel(
             nc.vector.tensor_copy(dst, window[:].indirect(offsets))
 
         def place_scale_rows(dst, src):
-            for i in range(4):
-                nc.sync.dma_start(dst[i:P:32, :].bitcast(I32), src[8 * i : P : 32, :].bitcast(I32))
+            for q in range(0, P, 32):
+                nc.sync.dma_start(dst[q : q + 4, :].bitcast(I32), src[q : q + 32 : 8, :].bitcast(I32))
 
-        d_bytes = zeroed_bytes("d_bytes", G)
-        x_bytes = zeroed_bytes("x_bytes", T)
+        def load_bytes(name, src):
+            rows, width = src.shape[1], src.shape[2]
+            tile = keep.tile([P, width], U8, name=name, align_bytes=64)
+            spread = src[0].bitcast(I32).unsqueeze(1).to_broadcast([rows, P // rows, width // 4])
+            nc.sync.dma_start(tile[:].bitcast(I32), spread)
+            return tile
+
+        d_bytes = load_bytes("d_bytes", d_scales)
         k1_list = load_list("k1_list", k1)
-        nc.scalar.dma_start(d_bytes[0:P:8, :].bitcast(I32), d_scales[0].bitcast(I32))
+        x_bytes = load_bytes("x_bytes", x_scales)
         offs_list = load_list("offs_list", offs)
-        for q in range(4):
-            nc.scalar.dma_start(
-                x_bytes[32 * q : 32 * q + 4, :].bitcast(I32), x_scales[0, 4 * q : 4 * q + 4, :].bitcast(I32)
-            )
+        x_table = load_words("x_table", x_words)
+        d_table = load_words("d_table", d_words)
         k2_list = load_list("k2_list", k2)
         k3_list = load_list("k3_list", k3)
         l1_list = load_list("l1_list", l1)
         r1_list = load_list("r1_list", r1)
-        x_table = load_words("x_table", x_words)
-        d_table = load_words("d_table", d_words)
         gain = keep.tile([P, PACK], F32, name="gain")
         nc.gpsimd.dma_start(gain[:], gs.rearrange("(p t) o -> p (t o)", t=PACK))
+        xq_scales = zeroed_bytes("xq_scales", S)
         w1_scales = zeroed_bytes("w1_scales", H)
         w23_scales = zeroed_bytes("w23_scales", 2 * H)
 
@@ -81,13 +84,14 @@ def tile_picked_pqtree_relu_p_kernel(
         cols = BANK // LANES
         w1_bytes = keep.tile([P, H], U8, name="w1_bytes", align_bytes=64)
         gather(w1_bytes[:], d_bytes, k1_list[:])
-        xq_scales0 = keep.tile([P, BANK], U8, name="xq_scales0", align_bytes=64)
-        gather(xq_scales0[:], x_bytes, offs_list[:, 0:cols])
+        xq_bytes = keep.tile([P, S], U8, name="xq_bytes", align_bytes=64)
+        gather(xq_bytes[:], x_bytes, offs_list[:])
         w1_bytes_dealt = keep.tile([P, H], U8, name="w1_bytes_dealt", align_bytes=64)
         nc.vector.tensor_copy(
             w1_bytes_dealt[:].rearrange("p (t m) -> p t m", t=PACK),
             w1_bytes[:].rearrange("p (m t) -> p t m", t=PACK),
         )
+        place_scale_rows(xq_scales, xq_bytes)
         place_scale_rows(w1_scales, w1_bytes_dealt)
         xq_words0 = keep.tile([P, BANK], U32, name="xq_words0", align_bytes=64)
         gather(xq_words0[:], x_table, offs_list[:, 0:cols])
@@ -99,11 +103,8 @@ def tile_picked_pqtree_relu_p_kernel(
             w1_dealt[:].rearrange("p (t m) -> p t m", t=PACK),
             w1_words[:].rearrange("p (m t) -> p t m", t=PACK),
         )
-        xq_scales1 = late.tile([P, BANK], U8, name="xq_scales1", align_bytes=64, offset=0)
-        xq_words1 = late.tile([P, BANK], U32, name="xq_words1", align_bytes=64, offset=BANK)
-        gather(xq_scales1[:], x_bytes, offs_list[:, cols : 2 * cols])
+        xq_words1 = late.tile([P, BANK], U32, name="xq_words1", align_bytes=64, offset=2 * H)
         gather(xq_words1[:], x_table, offs_list[:, cols : 2 * cols])
-        xq_scales = (xq_scales0, xq_scales1)
         xq_words = (xq_words0, xq_words1)
 
         weighted = [keep.tile([P, S], F32, name="weighted%d" % t, align_bytes=64) for t in range(PACK)]
@@ -116,7 +117,7 @@ def tile_picked_pqtree_relu_p_kernel(
                 lhsT=w1_dealt[:, m].bitcast(FP8X4),
                 lhsT_scale=w1_scales[:, m],
                 rhs=xq_words[j][:].bitcast(FP8X4),
-                rhs_scale=xq_scales[j][:],
+                rhs_scale=xq_scales[:, BANK * j : BANK * (j + 1)],
                 start=True,
                 stop=True,
             )
@@ -129,7 +130,7 @@ def tile_picked_pqtree_relu_p_kernel(
             first_product(t, j, ring.tile([P, BANK], F32, name="positive"))
         first_product(3, 1, keep.tile([P, BANK], F32, name="last_positive", tag="last_positive", align_bytes=64))
 
-        w23_bytes = keep.tile([P, 2 * H], U8, name="w23_bytes", tag="x_bytes", align_bytes=64)
+        w23_bytes = late.tile([P, 2 * H], U8, name="w23_bytes", align_bytes=64, offset=0)
         w23_words = keep.tile([P, 2 * H], U32, name="w23_words", tag="x_table", align_bytes=64)
         for a, lst in enumerate((k2_list, k3_list)):
             gather(w23_bytes[:, H * a : H * (a + 1)], d_bytes, lst[:])
@@ -139,11 +140,13 @@ def tile_picked_pqtree_relu_p_kernel(
 
         hcols = HALF // LANES
         left_planes = keep.tile([P, PACK, V], BF16, name="left_planes", tag="left_planes", align_bytes=64)
-        right_planes = keep.tile([P, PACK, HALF], BF16, name="right_planes", tag="last_positive", align_bytes=64)
+        right_planes = keep.tile([P, PACK, HALF], BF16, name="right_planes", tag="right_planes", align_bytes=64)
 
         def weave(name, planes):
             woven = keep.tile([P, HALF, PACK], BF16, name="woven_" + name, align_bytes=64)
-            nc.scalar.copy(woven[:], planes.rearrange("p t v -> p v t"))
+            nc.scalar.copy(
+                woven[:].rearrange("p (c i) t -> p c t i", i=4), planes.rearrange("p t (c i) -> p c t i", i=4)
+            )
             return woven
 
         def quantise(name, woven):
@@ -182,24 +185,23 @@ def tile_picked_pqtree_relu_p_kernel(
 
         for t in range(PACK):
             gather(left_planes[:, t, :], weighted[t], l1_list[:])
-        woven_l0 = weave("l0", left_planes[:, :, 0:HALF])
-        woven_l1 = weave("l1", left_planes[:, :, HALF:V])
-        for t in range(PACK):
             gather(right_planes[:, t, :], weighted[t], r1_list[:, 0:hcols])
+        woven_l0 = weave("l0", left_planes[:, :, 0:HALF])
         woven_r0 = weave("r0", right_planes[:])
-        second_pass(0, banks[0], quantise("l0", woven_l0))
-        second_pass(0, banks[1], quantise("l1", woven_l1))
+        woven_l1 = weave("l1", left_planes[:, :, HALF:V])
 
         woven_r1 = keep.tile([P, HALF, PACK], BF16, name="woven_r1", align_bytes=64)
-        low_planes = keep.tile([P, 2, HALF], BF16, name="low_planes", tag="left_planes", align_bytes=64)
+        low_planes = keep.tile([P, 2, HALF], BF16, name="low_planes", tag="last_positive", align_bytes=64)
         for t in range(2):
             gather(low_planes[:, t, :], weighted[t], r1_list[:, hcols : 2 * hcols])
         nc.scalar.copy(woven_r1[:, :, 0:2], low_planes[:].rearrange("p t v -> p v t"))
+        second_pass(0, banks[0], quantise("l0", woven_l0))
         second_pass(1, banks[0], quantise("r0", woven_r0))
-        high_planes = keep.tile([P, 2, HALF], BF16, name="high_planes", tag="last_positive", align_bytes=64)
+        high_planes = keep.tile([P, 2, HALF], BF16, name="high_planes", tag="right_planes", align_bytes=64)
         for t in range(2):
             gather(high_planes[:, t, :], weighted[2 + t], r1_list[:, hcols : 2 * hcols])
         finish(0, banks[0])
         nc.vector.tensor_copy(woven_r1[:, :, 2:4], high_planes[:].rearrange("p t v -> p v t"))
+        second_pass(0, banks[1], quantise("l1", woven_l1))
         second_pass(1, banks[1], quantise("r1", woven_r1))
         finish(1, banks[1])

@@ -1,6 +1,7 @@
 from contextlib import ExitStack
 
 import concourse.mybir as mybir
+from concourse.masks import make_identity
 
 K, T, S, V, G, H = 512, 2048, 1024, 512, 2048, 512
 FLOPS = 2 * K * H * S + 2 * 2 * H * H * V
@@ -30,18 +31,15 @@ def tile_picked_pqtree_relu_p_kernel(
         lists = ctx.enter_context(tc.tile_pool(name="lists", bufs=1))
         keep = ctx.enter_context(tc.tile_pool(name="keep", bufs=1))
         late = ctx.enter_context(tc.tile_pool(name="late", bufs=1))
-        ring = ctx.enter_context(tc.tile_pool(name="ring", bufs=2))
-        psum = ctx.enter_context(tc.psum_pool(name="psum", bufs=8))
+        psum = ctx.enter_context(tc.psum_pool(name="psum", bufs=1))
 
         def load_list(name, src):
             tile = lists.tile(list(src.shape), U16, name=name)
             nc.sync.dma_start(tile[:], src)
             return tile
 
-        def load_words(name, src):
-            tile = keep.tile([P, src.shape[2]], U32, name=name, tag=name, align_bytes=64)
+        def load_words(tile, src):
             nc.sync.dma_start(tile[:].bitcast(I32), src[0].rearrange("p n t -> p (n t)").bitcast(I32))
-            return tile
 
         def zeroed_bytes(name, width):
             tile = keep.tile([P, width], U8, name=name, tag=name, align_bytes=64)
@@ -64,74 +62,98 @@ def tile_picked_pqtree_relu_p_kernel(
 
         d_bytes = load_bytes("d_bytes", d_scales)
         k1_list = load_list("k1_list", k1)
-        x_bytes = load_bytes("x_bytes", x_scales)
+        x_bytes = keep.tile([P, T], U8, name="x_bytes", tag="x_bytes", align_bytes=64)
+        nc.vector.memset(x_bytes[:, 0 : T // 2].bitcast(I32), 0)
+        nc.gpsimd.memset(x_bytes[:, T // 2 : T].bitcast(I32), 0)
+        nc.scalar.dma_start(x_bytes[0:P:8, :].bitcast(I32), x_scales[0].bitcast(I32))
         offs_list = load_list("offs_list", offs)
-        x_table = load_words("x_table", x_words)
-        d_table = load_words("d_table", d_words)
         k2_list = load_list("k2_list", k2)
         k3_list = load_list("k3_list", k3)
         l1_list = load_list("l1_list", l1)
+        d_table = keep.tile([P, G], U32, name="d_table", align_bytes=64)
+        load_words(d_table, d_words)
+        x_table = late.tile([P, T], U32, name="x_table", align_bytes=64, offset=0)
+        load_words(x_table, x_words)
         r1_list = load_list("r1_list", r1)
-        gain = keep.tile([P, PACK], F32, name="gain")
+        gain = keep.tile([P, PACK], F32, name="gain", tag="gain", align_bytes=64)
         nc.gpsimd.dma_start(gain[:], gs.rearrange("(p t) o -> p (t o)", t=PACK))
-        xq_scales = zeroed_bytes("xq_scales", S)
-        w1_scales = zeroed_bytes("w1_scales", H)
+        identity = keep.tile([P, P], F32, name="identity")
+        make_identity(nc, identity[:])
+        first_scales = zeroed_bytes("first_scales", H + S)
         w23_scales = zeroed_bytes("w23_scales", 2 * H)
 
-        gain16 = keep.tile([P, PACK], F32, name="gain16")
-        nc.scalar.activation(gain16[:], gain[:], ACT.Copy, scale=0.0625)
-
         cols = BANK // LANES
-        w1_bytes = keep.tile([P, H], U8, name="w1_bytes", align_bytes=64)
-        gather(w1_bytes[:], d_bytes, k1_list[:])
-        xq_bytes = keep.tile([P, S], U8, name="xq_bytes", align_bytes=64)
-        gather(xq_bytes[:], x_bytes, offs_list[:])
-        w1_bytes_dealt = keep.tile([P, H], U8, name="w1_bytes_dealt", align_bytes=64)
-        nc.vector.tensor_copy(
-            w1_bytes_dealt[:].rearrange("p (t m) -> p t m", t=PACK),
-            w1_bytes[:].rearrange("p (m t) -> p t m", t=PACK),
-        )
-        place_scale_rows(xq_scales, xq_bytes)
-        place_scale_rows(w1_scales, w1_bytes_dealt)
-        xq_words0 = keep.tile([P, BANK], U32, name="xq_words0", align_bytes=64)
-        gather(xq_words0[:], x_table, offs_list[:, 0:cols])
-
-        w1_words = late.tile([P, H], U32, name="w1_words", align_bytes=64, offset=0)
+        first_bytes = keep.tile([P, H + S], U8, name="first_bytes", align_bytes=64)
+        gather(first_bytes[:, 0:H], d_bytes, k1_list[:])
+        gather(first_bytes[:, H : H + S], x_bytes, offs_list[:])
+        place_scale_rows(first_scales, first_bytes)
+        w1_words = keep.tile([P, H], U32, name="w1_words", tag="x_bytes", align_bytes=64)
         gather(w1_words[:], d_table, k1_list[:])
-        w1_dealt = keep.tile([P, H], U32, name="w1_dealt", align_bytes=64)
-        nc.vector.tensor_copy(
-            w1_dealt[:].rearrange("p (t m) -> p t m", t=PACK),
-            w1_words[:].rearrange("p (m t) -> p t m", t=PACK),
-        )
-        xq_words1 = late.tile([P, BANK], U32, name="xq_words1", align_bytes=64, offset=2 * H)
-        gather(xq_words1[:], x_table, offs_list[:, cols : 2 * cols])
-        xq_words = (xq_words0, xq_words1)
+        xq_words = keep.tile([P, S], U32, name="xq_words", align_bytes=64)
+        for j in range(S // BANK):
+            gather(xq_words[:, BANK * j : BANK * (j + 1)], x_table, offs_list[:, cols * j : cols * (j + 1)])
 
         weighted = [keep.tile([P, S], F32, name="weighted%d" % t, align_bytes=64) for t in range(PACK)]
+        positive = {}
 
-        def first_product(t, j, positive):
-            m = slice(P * t, P * (t + 1))
-            bank = psum.tile([P, BANK], F32, name="h_bank", tag="bank")
+        def bank_tile(n, width):
+            return psum.tile([P, width], F32, name="bank%d" % n, tag="bank%d" % n)
+
+        def rectify(n, bank, t0, t1):
+            part = keep.tile([P, t1 - t0, P], F32, name="positive%d_%d" % (n, t0), tag="positive%d" % n, align_bytes=64)
+            for t in range(t0, t1):
+                positive[n, t] = part[:, t - t0, :]
+            nc.scalar.activation(
+                part[:],
+                bank[:].rearrange("p (m t) -> p t m", t=PACK)[:, t0:t1, :],
+                ACT.Relu,
+                scale=0.0625,
+            )
+
+        def turn(t, free_banks):
+            for j, n in enumerate(free_banks):
+                bank = bank_tile(n, BANK)
+                for u in range(BANK // P):
+                    nc.tensor.transpose(
+                        bank[:, P * u : P * (u + 1)], positive[j * (BANK // P) + u, t], identity[:]
+                    )
+                nc.scalar.activation(
+                    weighted[t][:, BANK * j : BANK * (j + 1)], bank[:], ACT.Copy, scale=gain[:, t : t + 1]
+                )
+
+        warm_bank = bank_tile(7, H)
+        for n in range(3):
             nc.tensor.matmul_mx(
-                out=bank[:],
-                lhsT=w1_dealt[:, m].bitcast(FP8X4),
-                lhsT_scale=w1_scales[:, m],
-                rhs=xq_words[j][:].bitcast(FP8X4),
-                rhs_scale=xq_scales[:, BANK * j : BANK * (j + 1)],
+                out=warm_bank[:],
+                lhsT=w1_words[:, 0:P].bitcast(FP8X4),
+                lhsT_scale=first_bytes[:, 0:P],
+                rhs=w1_words[:].bitcast(FP8X4),
+                rhs_scale=first_bytes[:, 0:H],
                 start=True,
                 stop=True,
             )
-            nc.scalar.activation(positive[:], bank[:], ACT.Relu)
-            nc.scalar.activation(
-                weighted[t][:, BANK * j : BANK * (j + 1)], positive[:], ACT.Copy, scale=gain16[:, t : t + 1]
+
+        h_banks = [bank_tile(n, H) for n in range(S // P)]
+        for n, bank in enumerate(h_banks):
+            nc.tensor.matmul_mx(
+                out=bank[:],
+                lhsT=xq_words[:, P * n : P * (n + 1)].bitcast(FP8X4),
+                lhsT_scale=first_scales[:, H + P * n : H + P * (n + 1)],
+                rhs=w1_words[:].bitcast(FP8X4),
+                rhs_scale=first_scales[:, 0:H],
+                start=True,
+                stop=True,
             )
+            rectify(n, bank, 0, PACK if n < 2 else 2)
+        turn(0, (0, 1))
+        turn(1, (0, 1))
+        for n in range(2, S // P):
+            rectify(n, h_banks[n], 2, PACK)
+        turn(2, (0, 1))
+        turn(3, (2, 3))
 
-        for t, j in ((0, 0), (1, 0), (0, 1), (1, 1), (2, 0), (2, 1), (3, 0)):
-            first_product(t, j, ring.tile([P, BANK], F32, name="positive"))
-        first_product(3, 1, keep.tile([P, BANK], F32, name="last_positive", tag="last_positive", align_bytes=64))
-
-        w23_bytes = late.tile([P, 2 * H], U8, name="w23_bytes", align_bytes=64, offset=0)
-        w23_words = keep.tile([P, 2 * H], U32, name="w23_words", tag="x_table", align_bytes=64)
+        w23_bytes = late.tile([P, 2 * H], U8, name="w23_bytes", align_bytes=64, offset=8 * H)
+        w23_words = late.tile([P, 2 * H], U32, name="w23_words", align_bytes=64, offset=0)
         for a, lst in enumerate((k2_list, k3_list)):
             gather(w23_bytes[:, H * a : H * (a + 1)], d_bytes, lst[:])
         place_scale_rows(w23_scales, w23_bytes)
@@ -171,36 +193,37 @@ def tile_picked_pqtree_relu_p_kernel(
                 )
 
         def finish(b, banks):
-            for pair in range(2):
-                result = keep.tile([P, 2, HALF], F32, name="result%d%d" % (b, pair))
-                nc.scalar.activation(result[:, 0, :], banks[2 * pair][:], ACT.Copy, scale=0.0625)
-                if b == 0:
-                    nc.scalar.activation(result[:, 1, :], banks[2 * pair + 1][:], ACT.Copy, scale=0.0625)
+            for m, bank in enumerate(banks):
+                result = keep.tile([P, HALF], F32, name="result%d%d" % (b, m))
+                if b == 1 and m % 2 == 1:
+                    nc.vector.tensor_scalar(result[:], bank[:], 0.0625, None, ALU.mult)
                 else:
-                    nc.vector.tensor_scalar(result[:, 1, :], banks[2 * pair + 1][:], 0.0625, None, ALU.mult)
-                rows = out[2 * P * pair : 2 * P * (pair + 1), HALF * b : HALF * (b + 1)]
-                nc.sync.dma_start(rows.rearrange("(u p) v -> p u v", p=P), result[:])
+                    nc.scalar.activation(result[:], bank[:], ACT.Copy, scale=0.0625)
+                nc.sync.dma_start(out[P * m : P * (m + 1), HALF * b : HALF * (b + 1)], result[:])
 
-        banks = [[psum.tile([P, HALF], F32, name="o_bank", tag="bank") for m in range(4)] for b in range(2)]
+        banks = [[bank_tile(4 * (1 - b) + m, HALF) for m in range(4)] for b in range(2)]
 
+        low_planes = keep.tile([P, 2, HALF], BF16, name="low_planes", align_bytes=64)
         for t in range(PACK):
             gather(left_planes[:, t, :], weighted[t], l1_list[:])
             gather(right_planes[:, t, :], weighted[t], r1_list[:, 0:hcols])
-        woven_l0 = weave("l0", left_planes[:, :, 0:HALF])
-        woven_r0 = weave("r0", right_planes[:])
-        woven_l1 = weave("l1", left_planes[:, :, HALF:V])
-
-        woven_r1 = keep.tile([P, HALF, PACK], BF16, name="woven_r1", align_bytes=64)
-        low_planes = keep.tile([P, 2, HALF], BF16, name="low_planes", tag="last_positive", align_bytes=64)
-        for t in range(2):
-            gather(low_planes[:, t, :], weighted[t], r1_list[:, hcols : 2 * hcols])
-        nc.scalar.copy(woven_r1[:, :, 0:2], low_planes[:].rearrange("p t v -> p v t"))
-        second_pass(0, banks[0], quantise("l0", woven_l0))
-        second_pass(1, banks[0], quantise("r0", woven_r0))
-        high_planes = keep.tile([P, 2, HALF], BF16, name="high_planes", tag="right_planes", align_bytes=64)
+            if t < 2:
+                gather(low_planes[:, t, :], weighted[t], r1_list[:, hcols : 2 * hcols])
+        high_planes = keep.tile([P, 2, HALF], BF16, name="high_planes", tag="gain", align_bytes=64)
         for t in range(2):
             gather(high_planes[:, t, :], weighted[2 + t], r1_list[:, hcols : 2 * hcols])
+        woven_l0 = keep.tile([P, HALF, PACK], BF16, name="woven_l0", tag="positive4", align_bytes=64)
+        woven_l1 = keep.tile([P, HALF, PACK], BF16, name="woven_l1", tag="positive5", align_bytes=64)
+        nc.scalar.copy(woven_l0[:, :, 0:2], left_planes[:, 0:2, 0:HALF].rearrange("p t v -> p v t"))
+        nc.scalar.copy(woven_l1[:, :, 0:2], left_planes[:, 0:2, HALF:V].rearrange("p t v -> p v t"))
+        nc.scalar.copy(woven_l0[:, :, 2:4], left_planes[:, 2:4, 0:HALF].rearrange("p t v -> p v t"))
+        woven_r0 = weave("r0", right_planes[:])
+        nc.scalar.copy(woven_l1[:, :, 2:4], left_planes[:, 2:4, HALF:V].rearrange("p t v -> p v t"))
+        second_pass(0, banks[0], quantise("l0", woven_l0))
+        second_pass(1, banks[0], quantise("r0", woven_r0))
         finish(0, banks[0])
+        woven_r1 = keep.tile([P, HALF, PACK], BF16, name="woven_r1", tag="right_planes", align_bytes=64)
+        nc.vector.tensor_copy(woven_r1[:, :, 0:2], low_planes[:].rearrange("p t v -> p v t"))
         nc.vector.tensor_copy(woven_r1[:, :, 2:4], high_planes[:].rearrange("p t v -> p v t"))
         second_pass(0, banks[1], quantise("l1", woven_l1))
         second_pass(1, banks[1], quantise("r1", woven_r1))

from contextlib import ExitStack

import concourse.mybir as mybir
from concourse.masks import make_identity

K, T, S, V, G, H = 512, 2048, 1024, 512, 2048, 512
FLOPS = 2 * K * H * S + 2 * 2 * H * H * V

F32 = mybir.dt.float32
BF16 = mybir.dt.bfloat16
I32 = mybir.dt.int32
U32 = mybir.dt.uint32
U16 = mybir.dt.uint16
U8 = mybir.dt.uint8
FP8X4 = mybir.dt.float8_e4m3fn_x4
ACT = mybir.ActivationFunctionType
ALU = mybir.AluOpType

P = 128
PACK = 4
LANES = 16
BANK = 512
HALF = V // 2


def tile_picked_pqtree_relu_p_kernel(
    tc, x_words, x_scales, d_words, d_scales, gs, offs, k1, l1, r1, k2, k3, out
):
    nc = tc.nc
    with ExitStack() as ctx:
        lists = ctx.enter_context(tc.tile_pool(name="lists", bufs=1))
        keep = ctx.enter_context(tc.tile_pool(name="keep", bufs=1))
        late = ctx.enter_context(tc.tile_pool(name="late", bufs=1))
        psum = ctx.enter_context(tc.psum_pool(name="psum", bufs=1))

        def load_list(name, src):
            tile = lists.tile(list(src.shape), U16, name=name)
            nc.sync.dma_start(tile[:], src)
            return tile

        def load_words(tile, src):
            nc.sync.dma_start(tile[:].bitcast(I32), src[0].rearrange("p n t -> p (n t)").bitcast(I32))

        def zeroed_bytes(name, width):
            tile = keep.tile([P, width], U8, name=name, tag=name, align_bytes=64)
            nc.vector.memset(tile[:].bitcast(I32), 0)
            return tile

        def gather(dst, window, offsets):
            nc.vector.tensor_copy(dst, window[:].indirect(offsets))

        def place_scale_rows(dst, src):
            for q in range(0, P, 32):
                nc.sync.dma_start(dst[q : q + 4, :].bitcast(I32), src[q : q + 32 : 8, :].bitcast(I32))

        def load_bytes(name, src):
            rows, width = src.shape[1], src.shape[2]
            tile = keep.tile([P, width], U8, name=name, align_bytes=64)
            spread = src[0].bitcast(I32).unsqueeze(1).to_broadcast([rows, P // rows, width // 4])
            nc.sync.dma_start(tile[:].bitcast(I32), spread)
            return tile

        d_bytes = load_bytes("d_bytes", d_scales)
        k1_list = load_list("k1_list", k1)
        x_bytes = keep.tile([P, T], U8, name="x_bytes", tag="x_bytes", align_bytes=64)
        nc.vector.memset(x_bytes[:, 0 : T // 2].bitcast(I32), 0)
        nc.gpsimd.memset(x_bytes[:, T // 2 : T].bitcast(I32), 0)
        nc.scalar.dma_start(x_bytes[0:P:8, :].bitcast(I32), x_scales[0].bitcast(I32))
        offs_list = load_list("offs_list", offs)
        k2_list = load_list("k2_list", k2)
        k3_list = load_list("k3_list", k3)
        l1_list = load_list("l1_list", l1)
        d_table = keep.tile([P, G], U32, name="d_table", align_bytes=64)
        load_words(d_table, d_words)
        x_table = late.tile([P, T], U32, name="x_table", align_bytes=64, offset=0)
        load_words(x_table, x_words)
        r1_list = load_list("r1_list", r1)
        gain = keep.tile([P, PACK], F32, name="gain", tag="gain", align_bytes=64)
        nc.gpsimd.dma_start(gain[:], gs.rearrange("(p t) o -> p (t o)", t=PACK))
        identity = keep.tile([P, P], F32, name="identity")
        make_identity(nc, identity[:])
        first_scales = zeroed_bytes("first_scales", H + S)
        w23_scales = zeroed_bytes("w23_scales", 2 * H)

        cols = BANK // LANES
        first_bytes = keep.tile([P, H + S], U8, name="first_bytes", align_bytes=64)
        gather(first_bytes[:, 0:H], d_bytes, k1_list[:])
        gather(first_bytes[:, H : H + S], x_bytes, offs_list[:])
        place_scale_rows(first_scales, first_bytes)
        w1_words = keep.tile([P, H], U32, name="w1_words", tag="x_bytes", align_bytes=64)
        gather(w1_words[:], d_table, k1_list[:])
        xq_words = keep.tile([P, S], U32, name="xq_words", align_bytes=64)
        for j in range(S // BANK):
            gather(xq_words[:, BANK * j : BANK * (j + 1)], x_table, offs_list[:, cols * j : cols * (j + 1)])

        weighted = [keep.tile([P, S], F32, name="weighted%d" % t, align_bytes=64) for t in range(PACK)]
        positive = {}

        def bank_tile(n, width):
            return psum.tile([P, width], F32, name="bank%d" % n, tag="bank%d" % n)

        def rectify(n, bank, t0, t1):
            part = keep.tile([P, t1 - t0, P], F32, name="positive%d_%d" % (n, t0), tag="positive%d" % n, align_bytes=64)
            for t in range(t0, t1):
                positive[n, t] = part[:, t - t0, :]
            nc.scalar.activation(
                part[:],
                bank[:].rearrange("p (m t) -> p t m", t=PACK)[:, t0:t1, :],
                ACT.Relu,
                scale=0.0625,
            )

        def turn(t, free_banks):
            for j, n in enumerate(free_banks):
                bank = bank_tile(n, BANK)
                for u in range(BANK // P):
                    nc.tensor.transpose(
                        bank[:, P * u : P * (u + 1)], positive[j * (BANK // P) + u, t], identity[:]
                    )
                nc.scalar.activation(
                    weighted[t][:, BANK * j : BANK * (j + 1)], bank[:], ACT.Copy, scale=gain[:, t : t + 1]
                )

        warm_bank = bank_tile(7, H)
        for n in range(3):
            nc.tensor.matmul_mx(
                out=warm_bank[:],
                lhsT=w1_words[:, 0:P].bitcast(FP8X4),
                lhsT_scale=first_bytes[:, 0:P],
                rhs=w1_words[:].bitcast(FP8X4),
                rhs_scale=first_bytes[:, 0:H],
                start=True,
                stop=True,
            )

        h_banks = [bank_tile(n, H) for n in range(S // P)]
        for n, bank in enumerate(h_banks):
            nc.tensor.matmul_mx(
                out=bank[:],
                lhsT=xq_words[:, P * n : P * (n + 1)].bitcast(FP8X4),
                lhsT_scale=first_scales[:, H + P * n : H + P * (n + 1)],
                rhs=w1_words[:].bitcast(FP8X4),
                rhs_scale=first_scales[:, 0:H],
                start=True,
                stop=True,
            )
            rectify(n, bank, 0, PACK if n < 2 else 2)
        turn(0, (0, 1))
        turn(1, (0, 1))
        for n in range(2, S // P):
            rectify(n, h_banks[n], 2, PACK)
        turn(2, (0, 1))
        turn(3, (2, 3))

        w23_bytes = late.tile([P, 2 * H], U8, name="w23_bytes", align_bytes=64, offset=8 * H)
        w23_words = late.tile([P, 2 * H], U32, name="w23_words", align_bytes=64, offset=0)
        for a, lst in enumerate((k2_list, k3_list)):
            gather(w23_bytes[:, H * a : H * (a + 1)], d_bytes, lst[:])
        place_scale_rows(w23_scales, w23_bytes)
        for a, lst in enumerate((k2_list, k3_list)):
            gather(w23_words[:, H * a : H * (a + 1)], d_table, lst[:])

        hcols = HALF // LANES
        left_planes = keep.tile([P, PACK, V], BF16, name="left_planes", tag="left_planes", align_bytes=64)
        right_planes = keep.tile([P, PACK, HALF], BF16, name="right_planes", tag="right_planes", align_bytes=64)

        def weave(name, planes):
            woven = keep.tile([P, HALF, PACK], BF16, name="woven_" + name, align_bytes=64)
            nc.scalar.copy(
                woven[:].rearrange("p (c i) t -> p c t i", i=4), planes.rearrange("p t (c i) -> p c t i", i=4)
            )
            return woven

        def quantise(name, woven):
            words = keep.tile([P, HALF], U32, name="z_words_" + name, align_bytes=64)
            scales = keep.tile([P, HALF], U8, name="z_scales_" + name, align_bytes=64)
            nc.vector.quantize_mx(
                out=words[:].bitcast(FP8X4), scales=scales[:], in_=woven[:].rearrange("p v t -> p (v t)")
            )
            return words, scales

        def second_pass(a, banks, z):
            for m, bank in enumerate(banks):
                m0 = H * a + P * m
                nc.tensor.matmul_mx(
                    out=bank[:],
                    lhsT=w23_words[:, m0 : m0 + P].bitcast(FP8X4),
                    lhsT_scale=w23_scales[:, m0 : m0 + P],
                    rhs=z[0][:].bitcast(FP8X4),
                    rhs_scale=z[1][:],
                    start=(a == 0),
                    stop=(a == 1),
                )

        def finish(b, banks):
            for m, bank in enumerate(banks):
                result = keep.tile([P, HALF], F32, name="result%d%d" % (b, m))
                if b == 1 and m % 2 == 1:
                    nc.vector.tensor_scalar(result[:], bank[:], 0.0625, None, ALU.mult)
                else:
                    nc.scalar.activation(result[:], bank[:], ACT.Copy, scale=0.0625)
                nc.sync.dma_start(out[P * m : P * (m + 1), HALF * b : HALF * (b + 1)], result[:])

        banks = [[bank_tile(4 * (1 - b) + m, HALF) for m in range(4)] for b in range(2)]

        low_planes = keep.tile([P, 2, HALF], BF16, name="low_planes", align_bytes=64)
        for t in range(PACK):
            gather(left_planes[:, t, :], weighted[t], l1_list[:])
            gather(right_planes[:, t, :], weighted[t], r1_list[:, 0:hcols])
            if t < 2:
                gather(low_planes[:, t, :], weighted[t], r1_list[:, hcols : 2 * hcols])
        high_planes = keep.tile([P, 2, HALF], BF16, name="high_planes", tag="gain", align_bytes=64)
        for t in range(2):
            gather(high_planes[:, t, :], weighted[2 + t], r1_list[:, hcols : 2 * hcols])
        woven_l0 = keep.tile([P, HALF, PACK], BF16, name="woven_l0", tag="positive4", align_bytes=64)
        woven_l1 = keep.tile([P, HALF, PACK], BF16, name="woven_l1", tag="positive5", align_bytes=64)
        nc.scalar.copy(woven_l0[:, :, 0:2], left_planes[:, 0:2, 0:HALF].rearrange("p t v -> p v t"))
        nc.scalar.copy(woven_l1[:, :, 0:2], left_planes[:, 0:2, HALF:V].rearrange("p t v -> p v t"))
        nc.scalar.copy(woven_l0[:, :, 2:4], left_planes[:, 2:4, 0:HALF].rearrange("p t v -> p v t"))
        woven_r0 = weave("r0", right_planes[:])
        nc.scalar.copy(woven_l1[:, :, 2:4], left_planes[:, 2:4, HALF:V].rearrange("p t v -> p v t"))
        second_pass(0, banks[0], quantise("l0", woven_l0))
        second_pass(1, banks[0], quantise("r0", woven_r0))
        finish(0, banks[0])
        woven_r1 = keep.tile([P, HALF, PACK], BF16, name="woven_r1", tag="right_planes", align_bytes=64)
        nc.vector.tensor_copy(woven_r1[:, :, 0:2], low_planes[:].rearrange("p t v -> p v t"))
        nc.vector.tensor_copy(woven_r1[:, :, 2:4], high_planes[:].rearrange("p t v -> p v t"))
        second_pass(0, banks[1], quantise("l1", woven_l1))
        second_pass(1, banks[1], quantise("r1", woven_r1))
        finish(1, banks[1])
